import numpy as np, ml_dtypes
CORES = [242,247,114,119]
N = 4
NH, QP = 2, 128
def setup_inputs(rng):
    q = rng.standard_normal((N, 128, NH * QP), dtype=np.float32) / 4; k = rng.standard_normal((N, 128, NH * 128), dtype=np.float32)
    a = 2 * np.pi * rng.random((N, NH * QP)); s = 400 * rng.random((N, NH * QP)) ** 1.5; q[:, 0, :] = s * np.cos(a); q[:, 1, :] = s * np.sin(a); q[:, 2, :] = 150 * rng.standard_normal((N, NH * QP)); k[:, 2, :] = 1 + k[:, 2, :] / 50
    a = (2 * np.pi * rng.random((1, NH, 1)) + np.pi / 2 * (rng.permuted(np.tile(np.arange(N), (NH, 1)), axis=1).T.reshape(N, NH, 1) + 0.5) / N - 0.5 + rng.random((N, NH, 128))).reshape(N, NH * 128); k[:, 0, :] = np.cos(a); k[:, 1, :] = np.sin(a)
    return {"q": q.astype(ml_dtypes.bfloat16), "k": k.astype(ml_dtypes.bfloat16), "v": rng.standard_normal((N, 128, NH * 128), dtype=np.float32).astype(ml_dtypes.bfloat16)}
def setup_inputs_big(rng):
    d = setup_inputs(rng)
    for k in ("v",): d[k] = (d[k].astype(np.float32) * 1048576.0).astype(d[k].dtype)
    return d
def setup_inputs_small(rng):
    d = setup_inputs(rng)
    for k in ("v",): d[k] = (d[k].astype(np.float32) * (1 / 1048576.0)).astype(d[k].dtype)
    return d
def reference(q, k, v):
    Q, K, V = q.astype(np.float64), k.astype(np.float64), v.astype(np.float64)
    y = np.zeros((N, QP, NH * 128))
    for r in range(N):
        for h in range(NH):
            S = np.concatenate([K[j][:, 128 * h:128 * h + 128].T @ Q[r][:, QP * h:QP * h + QP] for j in range(N)], axis=0)
            P = np.exp(S - S.max(axis=0)); P = P / P.sum(axis=0)
            y[r][:, 128 * h:128 * h + 128] = P.T @ np.concatenate([V[j][:, 128 * h:128 * h + 128] for j in range(N)], axis=0)
    return {"y": y.astype(ml_dtypes.bfloat16)}

@@ -1,0 +1,232 @@
+from concourse.mybir import AluOpType, AxisListType, ActivationFunctionType
+
+NH = 2
+PIECES = ((0, 512),)
+SENDS = (("near", 0), ("chip", 0), ("far", 0))
+STAGES = (("own",), ("near",), ("chip",), ("far",))
+SLOT = {"chip": 0, "near": 1, "far": 2}
+NEV = 112
+
+SCRATCH = {
+    "qs": ("sbuf", [128, 256], "bfloat16"),
+    "kv": ("sbuf", [128, 512], "bfloat16"),
+    "land": ("sbuf", [128, 3 * 512], "bfloat16"),
+    "ones": ("sbuf", [128, 128], "bfloat16"),
+    "ident": ("sbuf", [128, 128], "bfloat16"),
+    "pw": ("sbuf", [128, NH * 512], "bfloat16"),
+    "pt": ("sbuf", [128, NH * 512], "bfloat16"),
+    "dg": ("sbuf", [128, NH * 512], "bfloat16"),
+    "ob": ("sbuf", [128, NH * 512], "bfloat16"),
+    "st": ("sbuf", [128, 48], "float32"),
+    "ysb": ("sbuf", [128, 256], "bfloat16"),
+    "s00": ("psum", [128, 512], "float32"),
+    "s01": ("psum", [128, 512], "float32"),
+    "s10": ("psum", [128, 512], "float32"),
+    "s11": ("psum", [128, 512], "float32"),
+    "t0": ("psum", [128, 1024], "bfloat16"),
+    "t1": ("psum", [128, 1024], "bfloat16"),
+    "o0": ("psum", [128, 512], "float32"),
+    "o1": ("psum", [128, 512], "float32"),
+}
+SEMAPHORES = ["sent"] + ["arr%d%d" % (j, p) for j in range(3) for p in range(2)] + ["e%d" % i for i in range(NEV)]
+
+
+def rank_program(g, core, T, topo):
+    if T.rank_of(core) is None:
+        return
+    EXP, IDN = ActivationFunctionType.Exp, ActivationFunctionType.Identity
+    MUL, MAX = AluOpType.mult, AluOpType.max
+
+    def same_chip(a, b):
+        return (topo.host(a), topo.chip(a)) == (topo.host(b), topo.chip(b))
+
+    def place(src, dst):
+        if same_chip(src, dst):
+            return "chip"
+        return "near" if topo.die(src) == topo.die(dst) else "far"
+
+    def engines(src, dst):
+        m = topo.mask(src, dst)
+        if same_chip(src, dst):
+            off = 0
+            for d in T.cores:
+                if not same_chip(src, d):
+                    off |= topo.mask(src, d)
+            m = (m & ~off) or m
+        return m
+
+    def count(m):
+        return bin(m).count("1")
+
+    peer = {place(core, d): d for d in T.cores if d != core}
+
+    queues = {"pe": g.tensor, "dve": g.vector, "act": g.scalar, "sp": g.sync, "g": g}
+    ops, evs = [], []
+
+    def ev(val, sem=None):
+        e = {"n": len(evs), "val": val, "sem": sem, "used": False}
+        evs.append(e)
+        return e
+
+    def op(q, fn, waits=(), sig=None, inc=1):
+        ops.append((q, fn, [w for w in waits if w is not None], sig, inc))
+
+    def mm(out, lhsT, rhs, start, stop):
+        return lambda: g.tensor.matmul(out, lhsT, rhs, start, stop)
+
+    def tr(out, in_):
+        return lambda: g.tensor.transpose(out, in_, T.ident[:])
+
+    def tsc(out, in0, s1):
+        return lambda: g.vector.tensor_scalar(out, in0, s1, None, MUL)
+
+    def cpy(out, in_):
+        return lambda: g.vector.tensor_copy(out, in_)
+
+    def actv(out, in_, func, bias, scale, acc=None):
+        return lambda: g.scalar.activation(out, in_, func, bias=bias, scale=scale, accum_out=acc)
+
+    def col(kind, s, h):
+        c = 8 * kind + 2 * s + h
+        return T.st[:, c:c + 1]
+
+    ld_k, ld_v, ld_q = ev(16), ev(16), ev(16)
+    op("sp", lambda: g.sync.dma_start(T.kv[:, 0:256], T.k[:, :]), sig=ld_k, inc=16)
+    op("act", lambda: g.scalar.dma_start(T.kv[:, 256:512], T.v[:, :]), sig=ld_v, inc=16)
+    op("sp", lambda: g.sync.dma_start(T.qs[:], T.q[:, :]), sig=ld_q, inc=16)
+
+    e_ones, e_id = ev(1), ev(1)
+    op("dve", lambda: g.vector.memset(T.ones[:], 1.0), sig=e_ones)
+    op("g", lambda: g.affine_select(T.ident[:], T.ones[:], [[-1, 128]], AluOpType.is_equal, 0.0, 0, 1), [e_ones], e_id)
+
+    def send(where, p):
+        d = peer[where]
+        rid, pid = topo.addr(d, core)
+        a, b = PIECES[p]
+        j = SLOT[where]
+        return lambda: g.remote_dma(T.land[:, 512 * j + a:512 * j + b], T.kv[:, a:b], T.sem["arr%d%d" % (j, p)],
+                                    T.sem.sent, pid, rid, engines(core, d))
+
+    total = 0
+    for where, p in SENDS:
+        a, b = PIECES[p]
+        op("g", send(where, p), [ld_k if a < 256 else None, ld_v if b > 256 else None])
+        total += count(engines(core, peer[where]))
+    e_sent = ev(total, T.sem.sent)
+
+    arr = {(w, p): ev(count(engines(peer[w], core)), T.sem["arr%d%d" % (SLOT[w], p)]) for w, p in SENDS}
+
+    def piece_of(c):
+        return [p for p, (a, b) in enumerate(PIECES) if a <= c < b][0]
+
+    def k_of(b, h):
+        if b == "own":
+            return T.kv[:, 128 * h:128 * h + 128], ld_k
+        o = 512 * SLOT[b] + 128 * h
+        return T.land[:, o:o + 128], arr[b, piece_of(128 * h)]
+
+    def v_of(b, h):
+        if b == "own":
+            return T.kv[:, 256 + 128 * h:384 + 128 * h], ld_v
+        o = 512 * SLOT[b] + 256 + 128 * h
+        return T.land[:, o:o + 128], arr[b, piece_of(256 + 128 * h)]
+
+    H = range(NH)
+    TB = [T.t0, T.t1]
+    OB = [T.o0, T.o1]
+    e_max, e_mcol, e_exp, e_cp, e_ob, e_l = {}, {}, {}, {}, {}, {}
+    nst = len(STAGES)
+    pos = 0
+    for s, blocks in enumerate(STAGES):
+        nb, last = len(blocks), s == nst - 1
+        w = 128 * nb
+        SB = [T["s%d%d" % (s % 2, h)] for h in H]
+        e_st, e_f, e_t, e_dg, e_o = {}, {}, {}, {}, {}
+        for h in H:
+            e_st[h] = ev(nb)
+            for i, b in enumerate(blocks):
+                ap, e = k_of(b, h)
+                op("pe", mm(SB[h][:, 128 * i:128 * i + 128], T.qs[:, 128 * h:128 * h + 128], ap, True, True),
+                   [ld_q, e, e_mcol.get((s - 1, h))], e_st[h])
+        for h in H:
+            e_max[s, h] = ev(1)
+            op("dve", (lambda o, i: lambda: g.vector.tensor_reduce(o, i, AxisListType.X, MAX, negate=True))(
+                col(0, s, h), SB[h][:, 0:w + (1 if s else 0)]), [e_st[h], e_mcol.get((s - 1, h))], e_max[s, h])
+        if not last:
+            nw = 128 * len(STAGES[s + 1])
+            for h in H:
+                e_mcol[s, h] = ev(1)
+                op("dve", tsc(T["s%d%d" % ((s + 1) % 2, h)][:, nw:nw + 1], col(0, s, h), -1.0),
+                   [e_max[s, h], e_exp.get((s - 1, h))], e_mcol[s, h])
+        for h in H:
+            e_exp[s, h] = ev(1)
+            o = 512 * h + pos
+            op("act", actv(T.pw[:, o:o + w], SB[h][:, 0:w], EXP, col(0, s, h), 1.0, col(1 if s else 3, s, h)),
+               [e_max[s, h]], e_exp[s, h])
+        if s:
+            for h in H:
+                e_f[h] = ev(1)
+                op("act", actv(col(2, s, h), col(0, s - 1, h), EXP, col(0, s, h), -1.0), [e_max[s, h], e_max[s - 1, h]], e_f[h])
+            for h in H:
+                e_l[s, h] = ev(1)
+                op("act", actv(col(3, s, h), col(3, s - 1, h), IDN, col(1, s, h), col(2, s, h)),
+                   [e_f[h], e_exp[s, h], e_l[s - 1, h]], e_l[s, h])
+        else:
+            for h in H:
+                e_l[s, h] = e_exp[s, h]
+        for h in H:
+            e_t[h] = ev(nb)
+            for i in range(nb):
+                o = 512 * h + pos + 128 * i
+                op("pe", tr(TB[h][:, 128 * i:128 * i + 128], T.pw[:, o:o + 128]), [e_exp[s, h], e_id, e_cp.get((s - 1, h))], e_t[h])
+        for h in H:
+            e_cp[s, h] = ev(1)
+            o = 512 * h + pos
+            op("dve", cpy(T.pt[:, o:o + w], TB[h][:, 0:w]), [e_t[h]], e_cp[s, h])
+            if s:
+                e_dg[h] = ev(1)
+                o = 512 * h + 128 * s
+                op("dve", tsc(T.dg[:, o:o + 128], T.ident[:], col(2, s, h)), [e_f[h], e_id], e_dg[h])
+        for h in H:
+            e_o[h] = ev(nb + (1 if s else 0))
+            if s:
+                o = 512 * h + 128 * s
+                op("pe", mm(OB[h][:, 0:128], T.dg[:, o:o + 128], T.ob[:, o - 128:o], True, False), [e_dg[h], e_ob[s - 1, h]], e_o[h])
+            for i, b in enumerate(blocks):
+                ap, e = v_of(b, h)
+                o = 512 * h + pos + 128 * i
+                op("pe", mm(OB[h][:, 0:128], T.pt[:, o:o + 128], ap, s == 0 and i == 0, i == nb - 1), [e_cp[s, h], e], e_o[h])
+        if not last:
+            for h in H:
+                e_ob[s, h] = ev(1)
+                o = 512 * h + 128 * s
+                op("dve", cpy(T.ob[:, o:o + 128], OB[h][:, 0:128]), [e_o[h]], e_ob[s, h])
+        else:
+            e_r, e_y0, e_y1, e_done = ev(1), ev(1), ev(1), ev(16)
+            c = 24 + 2 * s
+            op("dve", lambda: g.vector.reciprocal(T.st[:, 40:42], T.st[:, c:c + 2]), [e_l[s, 0], e_l[s, 1]], e_r)
+            op("act", actv(T.ysb[:, 0:128], OB[0][:, 0:128], IDN, 0.0, T.st[:, 40:41]), [e_o[0], e_r], e_y0)
+            op("dve", tsc(T.ysb[:, 128:256], OB[1][:, 0:128], T.st[:, 41:42]), [e_o[1], e_r], e_y1)
+            op("sp", lambda: g.sync.dma_start(T.y[:, :], T.ysb[:]), [e_y0, e_y1], e_done, 16)
+            op("sp", None, [e_done])
+        pos += w
+    op("g", None, [e_sent])
+
+    for _, _, waits, _, _ in ops:
+        for e in waits:
+            e["used"] = True
+    free = [0]
+    for e in evs:
+        if e["used"] and e["sem"] is None:
+            e["sem"] = T.sem["e%d" % free[0]]
+            free[0] += 1
+    seen = set()
+    for q, fn, waits, sig, inc in ops:
+        for e in waits:
+            if (q, e["n"]) not in seen:
+                seen.add((q, e["n"]))
+                queues[q].wait_ge(e["sem"], e["val"])
+        if fn is not None:
+            ins = fn()
+            if sig is not None and sig["used"]:
+                ins.then_inc(sig["sem"], inc)

@@ -1,9 +1,10 @@
+from concourse.bass import DstId, RemoteDMATransfer
 from concourse.mybir import AluOpType, AxisListType, ActivationFunctionType
 
 NH = 2
 PIECES = ((0, 512),)
-SENDS = (("near", 0), ("chip", 0), ("far", 0))
-STAGES = (("own",), ("near",), ("chip",), ("far",))
+SENDS = ((("near", 0), ("chip", 0)), (("far", 0),))
+STAGES = (("own",), ("chip", "near"), ("far",))
 SLOT = {"chip": 0, "near": 1, "far": 2}
 NEV = 112
 
@@ -99,22 +100,30 @@ def rank_program(g, core, T, topo):
     op("dve", lambda: g.vector.memset(T.ones[:], 1.0), sig=e_ones)
     op("g", lambda: g.affine_select(T.ident[:], T.ones[:], [[-1, 128]], AluOpType.is_equal, 0.0, 0, 1), [e_ones], e_id)
 
-    def send(where, p):
-        d = peer[where]
-        rid, pid = topo.addr(d, core)
-        a, b = PIECES[p]
-        j = SLOT[where]
-        return lambda: g.remote_dma(T.land[:, 512 * j + a:512 * j + b], T.kv[:, a:b], T.sem["arr%d%d" % (j, p)],
-                                    T.sem.sent, pid, rid, engines(core, d))
+    def send(call):
+        parts = []
+        for where, p in call:
+            d = peer[where]
+            rid, pid = topo.addr(d, core)
+            a, b = PIECES[p]
+            j = SLOT[where]
+            parts.append((T.land[:, 512 * j + a:512 * j + b], T.kv[:, a:b], T.sem["arr%d%d" % (j, p)], pid, rid, engines(core, d)))
+        if len(parts) == 1:
+            o, i, sem, pid, rid, m = parts[0]
+            return lambda: g.remote_dma(o, i, sem, T.sem.sent, pid, rid, m)
+        return lambda: g.remote_dma_fused(
+            [RemoteDMATransfer(dst_ids=[DstId(rid=rid, pnc=pid)], dma_engine_mask=m, remote_sem=sem, src=i, dst=o)
+             for o, i, sem, pid, rid, m in parts], local_sem=T.sem.sent)
 
     total = 0
-    for where, p in SENDS:
-        a, b = PIECES[p]
-        op("g", send(where, p), [ld_k if a < 256 else None, ld_v if b > 256 else None])
-        total += count(engines(core, peer[where]))
+    for call in SENDS:
+        lo = min(PIECES[p][0] for _, p in call)
+        hi = max(PIECES[p][1] for _, p in call)
+        op("g", send(call), [ld_k if lo < 256 else None, ld_v if hi > 256 else None])
+        total += sum(count(engines(core, peer[where])) for where, _ in call)
     e_sent = ev(total, T.sem.sent)
 
-    arr = {(w, p): ev(count(engines(peer[w], core)), T.sem["arr%d%d" % (SLOT[w], p)]) for w, p in SENDS}
+    arr = {(w, p): ev(count(engines(peer[w], core)), T.sem["arr%d%d" % (SLOT[w], p)]) for call in SENDS for w, p in call}
 
     def piece_of(c):
         return [p for p, (a, b) in enumerate(PIECES) if a <= c < b][0]
@@ -134,14 +143,14 @@ def rank_program(g, core, T, topo):
     H = range(NH)
     TB = [T.t0, T.t1]
     OB = [T.o0, T.o1]
-    e_max, e_mcol, e_exp, e_cp, e_ob, e_l = {}, {}, {}, {}, {}, {}
+    e_max, e_mcol, e_exp, e_cp, e_ob, e_l, e_o = {}, {}, {}, {}, {}, {}, {}
     nst = len(STAGES)
     pos = 0
     for s, blocks in enumerate(STAGES):
         nb, last = len(blocks), s == nst - 1
         w = 128 * nb
         SB = [T["s%d%d" % (s % 2, h)] for h in H]
-        e_st, e_f, e_t, e_dg, e_o = {}, {}, {}, {}, {}
+        e_st, e_f, e_t, e_dg = {}, {}, {}, {}
         for h in H:
             e_st[h] = ev(nb)
             for i, b in enumerate(blocks):
@@ -188,25 +197,25 @@ def rank_program(g, core, T, topo):
                 o = 512 * h + 128 * s
                 op("dve", tsc(T.dg[:, o:o + 128], T.ident[:], col(2, s, h)), [e_f[h], e_id], e_dg[h])
         for h in H:
-            e_o[h] = ev(nb + (1 if s else 0))
+            e_o[s, h] = ev(nb + (1 if s else 0))
             if s:
                 o = 512 * h + 128 * s
-                op("pe", mm(OB[h][:, 0:128], T.dg[:, o:o + 128], T.ob[:, o - 128:o], True, False), [e_dg[h], e_ob[s - 1, h]], e_o[h])
+                op("pe", mm(OB[h][:, 0:128], T.dg[:, o:o + 128], T.ob[:, o - 128:o], True, False), [e_dg[h], e_ob[s - 1, h]], e_o[s, h])
             for i, b in enumerate(blocks):
                 ap, e = v_of(b, h)
                 o = 512 * h + pos + 128 * i
-                op("pe", mm(OB[h][:, 0:128], T.pt[:, o:o + 128], ap, s == 0 and i == 0, i == nb - 1), [e_cp[s, h], e], e_o[h])
+                op("pe", mm(OB[h][:, 0:128], T.pt[:, o:o + 128], ap, s == 0 and i == 0, i == nb - 1), [e_cp[s, h], e], e_o[s, h])
         if not last:
             for h in H:
                 e_ob[s, h] = ev(1)
                 o = 512 * h + 128 * s
-                op("dve", cpy(T.ob[:, o:o + 128], OB[h][:, 0:128]), [e_o[h]], e_ob[s, h])
+                op("dve", cpy(T.ob[:, o:o + 128], OB[h][:, 0:128]), [e_o[s, h]], e_ob[s, h])
         else:
             e_r, e_y0, e_y1, e_done = ev(1), ev(1), ev(1), ev(16)
             c = 24 + 2 * s
             op("dve", lambda: g.vector.reciprocal(T.st[:, 40:42], T.st[:, c:c + 2]), [e_l[s, 0], e_l[s, 1]], e_r)
-            op("act", actv(T.ysb[:, 0:128], OB[0][:, 0:128], IDN, 0.0, T.st[:, 40:41]), [e_o[0], e_r], e_y0)
-            op("dve", tsc(T.ysb[:, 128:256], OB[1][:, 0:128], T.st[:, 41:42]), [e_o[1], e_r], e_y1)
+            op("act", actv(T.ysb[:, 0:128], OB[0][:, 0:128], IDN, 0.0, T.st[:, 40:41]), [e_o[s, 0], e_r], e_y0)
+            op("dve", tsc(T.ysb[:, 128:256], OB[1][:, 0:128], T.st[:, 41:42]), [e_o[s, 1], e_r], e_y1)
             op("sp", lambda: g.sync.dma_start(T.y[:, :], T.ysb[:]), [e_y0, e_y1], e_done, 16)
             op("sp", None, [e_done])
         pos += w

@@ -5,6 +5,7 @@ NH = 2
 PIECES = ((0, 512),)
 SENDS = ((("near", 0), ("chip", 0)), (("far", 0),))
 STAGES = (("own",), ("chip", "near"), ("far",))
+ORDER = (("f", 0), ("t", 0), ("b", 0), ("f", 1), ("t", 1), ("f", 2), ("b", 1), ("t", 2), ("b", 2))
 SLOT = {"chip": 0, "near": 1, "far": 2}
 NEV = 112
 
@@ -143,25 +144,26 @@ def rank_program(g, core, T, topo):
     H = range(NH)
     TB = [T.t0, T.t1]
     OB = [T.o0, T.o1]
-    e_max, e_mcol, e_exp, e_cp, e_ob, e_l, e_o = {}, {}, {}, {}, {}, {}, {}
+    e_st, e_max, e_mcol, e_exp, e_f, e_l, e_t, e_cp, e_dg, e_o, e_ob = {}, {}, {}, {}, {}, {}, {}, {}, {}, {}, {}
     nst = len(STAGES)
-    pos = 0
-    for s, blocks in enumerate(STAGES):
-        nb, last = len(blocks), s == nst - 1
+    POS = [128 * sum(len(STAGES[i]) for i in range(s)) for s in range(nst)]
+
+    def front(s):
+        blocks = STAGES[s]
+        nb, pos = len(blocks), POS[s]
         w = 128 * nb
         SB = [T["s%d%d" % (s % 2, h)] for h in H]
-        e_st, e_f, e_t, e_dg = {}, {}, {}, {}
         for h in H:
-            e_st[h] = ev(nb)
+            e_st[s, h] = ev(nb)
             for i, b in enumerate(blocks):
                 ap, e = k_of(b, h)
                 op("pe", mm(SB[h][:, 128 * i:128 * i + 128], T.qs[:, 128 * h:128 * h + 128], ap, True, True),
-                   [ld_q, e, e_mcol.get((s - 1, h))], e_st[h])
+                   [ld_q, e, e_mcol.get((s - 1, h))], e_st[s, h])
         for h in H:
             e_max[s, h] = ev(1)
             op("dve", (lambda o, i: lambda: g.vector.tensor_reduce(o, i, AxisListType.X, MAX, negate=True))(
-                col(0, s, h), SB[h][:, 0:w + (1 if s else 0)]), [e_st[h], e_mcol.get((s - 1, h))], e_max[s, h])
-        if not last:
+                col(0, s, h), SB[h][:, 0:w + (1 if s else 0)]), [e_st[s, h], e_mcol.get((s - 1, h))], e_max[s, h])
+        if s < nst - 1:
             nw = 128 * len(STAGES[s + 1])
             for h in H:
                 e_mcol[s, h] = ev(1)
@@ -174,38 +176,47 @@ def rank_program(g, core, T, topo):
                [e_max[s, h]], e_exp[s, h])
         if s:
             for h in H:
-                e_f[h] = ev(1)
-                op("act", actv(col(2, s, h), col(0, s - 1, h), EXP, col(0, s, h), -1.0), [e_max[s, h], e_max[s - 1, h]], e_f[h])
+                e_f[s, h] = ev(1)
+                op("act", actv(col(2, s, h), col(0, s - 1, h), EXP, col(0, s, h), -1.0), [e_max[s, h], e_max[s - 1, h]], e_f[s, h])
             for h in H:
                 e_l[s, h] = ev(1)
                 op("act", actv(col(3, s, h), col(3, s - 1, h), IDN, col(1, s, h), col(2, s, h)),
-                   [e_f[h], e_exp[s, h], e_l[s - 1, h]], e_l[s, h])
+                   [e_f[s, h], e_exp[s, h], e_l[s - 1, h]], e_l[s, h])
         else:
             for h in H:
                 e_l[s, h] = e_exp[s, h]
+
+    def turn(s):
+        nb, pos = len(STAGES[s]), POS[s]
+        w = 128 * nb
         for h in H:
-            e_t[h] = ev(nb)
+            e_t[s, h] = ev(nb)
             for i in range(nb):
                 o = 512 * h + pos + 128 * i
-                op("pe", tr(TB[h][:, 128 * i:128 * i + 128], T.pw[:, o:o + 128]), [e_exp[s, h], e_id, e_cp.get((s - 1, h))], e_t[h])
+                op("pe", tr(TB[h][:, 128 * i:128 * i + 128], T.pw[:, o:o + 128]), [e_exp[s, h], e_id, e_cp.get((s - 1, h))], e_t[s, h])
         for h in H:
             e_cp[s, h] = ev(1)
             o = 512 * h + pos
-            op("dve", cpy(T.pt[:, o:o + w], TB[h][:, 0:w]), [e_t[h]], e_cp[s, h])
+            op("dve", cpy(T.pt[:, o:o + w], TB[h][:, 0:w]), [e_t[s, h]], e_cp[s, h])
             if s:
-                e_dg[h] = ev(1)
+                e_dg[s, h] = ev(1)
                 o = 512 * h + 128 * s
-                op("dve", tsc(T.dg[:, o:o + 128], T.ident[:], col(2, s, h)), [e_f[h], e_id], e_dg[h])
+                op("dve", tsc(T.dg[:, o:o + 128], T.ident[:], col(2, s, h)), [e_f[s, h], e_id], e_dg[s, h])
+
+    def back(s):
+        blocks = STAGES[s]
+        nb, pos = len(blocks), POS[s]
         for h in H:
             e_o[s, h] = ev(nb + (1 if s else 0))
             if s:
                 o = 512 * h + 128 * s
-                op("pe", mm(OB[h][:, 0:128], T.dg[:, o:o + 128], T.ob[:, o - 128:o], True, False), [e_dg[h], e_ob[s - 1, h]], e_o[s, h])
+                op("pe", mm(OB[h][:, 0:128], T.dg[:, o:o + 128], T.ob[:, o - 128:o], True, False),
+                   [e_dg[s, h], e_ob[s - 1, h]], e_o[s, h])
             for i, b in enumerate(blocks):
                 ap, e = v_of(b, h)
                 o = 512 * h + pos + 128 * i
                 op("pe", mm(OB[h][:, 0:128], T.pt[:, o:o + 128], ap, s == 0 and i == 0, i == nb - 1), [e_cp[s, h], e], e_o[s, h])
-        if not last:
+        if s < nst - 1:
             for h in H:
                 e_ob[s, h] = ev(1)
                 o = 512 * h + 128 * s
@@ -218,7 +229,10 @@ def rank_program(g, core, T, topo):
             op("dve", tsc(T.ysb[:, 128:256], OB[1][:, 0:128], T.st[:, 41:42]), [e_o[s, 1], e_r], e_y1)
             op("sp", lambda: g.sync.dma_start(T.y[:, :], T.ysb[:]), [e_y0, e_y1], e_done, 16)
             op("sp", None, [e_done])
-        pos += w
+
+    part = {"f": front, "t": turn, "b": back}
+    for name, s in ORDER:
+        part[name](s)
     op("g", None, [e_sent])
 
     for _, _, waits, _, _ in ops:

@@ -2,10 +2,10 @@ from concourse.bass import DstId, RemoteDMATransfer
 from concourse.mybir import AluOpType, AxisListType, ActivationFunctionType
 
 NH = 2
-PIECES = ((0, 512),)
-SENDS = ((("near", 0), ("chip", 0)), (("far", 0),))
-STAGES = (("own",), ("chip", "near"), ("far",))
-ORDER = (("f", 0), ("t", 0), ("b", 0), ("f", 1), ("t", 1), ("f", 2), ("b", 1), ("t", 2), ("b", 2))
+PIECES = ((0, 256), (256, 512))
+SENDS = ((("near", 0), ("far", 0), ("chip", 0)), (("near", 1), ("far", 1), ("chip", 1)))
+STAGES = (("own",), ("chip",), ("near", "far"))
+ORDER = (("f", 0), ("t", 0), ("f", 1), ("b", 0), ("t", 1), ("f", 2), ("b", 1), ("t", 2), ("b", 2))
 SLOT = {"chip": 0, "near": 1, "far": 2}
 NEV = 112
 
@@ -30,7 +30,7 @@ SCRATCH = {
     "o0": ("psum", [128, 512], "float32"),
     "o1": ("psum", [128, 512], "float32"),
 }
-SEMAPHORES = ["sent"] + ["arr%d%d" % (j, p) for j in range(3) for p in range(2)] + ["e%d" % i for i in range(NEV)]
+SEMAPHORES = ["sent"] + ["arr%d%d" % (j, p) for j in range(3) for p in range(3)] + ["e%d" % i for i in range(NEV)]
 
 
 def rank_program(g, core, T, topo):
@@ -54,8 +54,10 @@ def rank_program(g, core, T, topo):
             for d in T.cores:
                 if not same_chip(src, d):
                     off |= topo.mask(src, d)
-            m = (m & ~off) or m
-        return m
+            return (m & ~off) or m
+        bits = [1 << i for i in range(m.bit_length()) if (m >> i) & 1]
+        half = len(bits) // 2
+        return sum(bits[:half] if place(src, dst) == "near" else bits[half:])
 
     def count(m):
         return bin(m).count("1")
@@ -94,8 +96,8 @@ def rank_program(g, core, T, topo):
 
     ld_k, ld_v, ld_q = ev(16), ev(16), ev(16)
     op("sp", lambda: g.sync.dma_start(T.kv[:, 0:256], T.k[:, :]), sig=ld_k, inc=16)
-    op("act", lambda: g.scalar.dma_start(T.kv[:, 256:512], T.v[:, :]), sig=ld_v, inc=16)
     op("sp", lambda: g.sync.dma_start(T.qs[:], T.q[:, :]), sig=ld_q, inc=16)
+    op("sp", lambda: g.sync.dma_start(T.kv[:, 256:512], T.v[:, :]), sig=ld_v, inc=16)
 
     e_ones, e_id = ev(1), ev(1)
     op("dve", lambda: g.vector.memset(T.ones[:], 1.0), sig=e_ones)
@@ -126,20 +128,20 @@ def rank_program(g, core, T, topo):
 
     arr = {(w, p): ev(count(engines(peer[w], core)), T.sem["arr%d%d" % (SLOT[w], p)]) for call in SENDS for w, p in call}
 
-    def piece_of(c):
-        return [p for p, (a, b) in enumerate(PIECES) if a <= c < b][0]
+    def landed(b, c):
+        return [e for (w, p), e in arr.items() if w == b and PIECES[p][0] <= c < PIECES[p][1]][0]
 
     def k_of(b, h):
         if b == "own":
             return T.kv[:, 128 * h:128 * h + 128], ld_k
         o = 512 * SLOT[b] + 128 * h
-        return T.land[:, o:o + 128], arr[b, piece_of(128 * h)]
+        return T.land[:, o:o + 128], landed(b, 128 * h)
 
     def v_of(b, h):
         if b == "own":
             return T.kv[:, 256 + 128 * h:384 + 128 * h], ld_v
         o = 512 * SLOT[b] + 256 + 128 * h
-        return T.land[:, o:o + 128], arr[b, piece_of(256 + 128 * h)]
+        return T.land[:, o:o + 128], landed(b, 256 + 128 * h)
 
     H = range(NH)
     TB = [T.t0, T.t1]

from concourse.bass import DstId, RemoteDMATransfer
from concourse.mybir import AluOpType, AxisListType, ActivationFunctionType

NH = 2
PIECES = ((0, 256), (256, 512))
SENDS = ((("near", 0), ("far", 0), ("chip", 0)), (("near", 1), ("far", 1), ("chip", 1)))
STAGES = (("own",), ("chip",), ("near", "far"))
ORDER = (("f", 0), ("t", 0), ("f", 1), ("b", 0), ("t", 1), ("f", 2), ("b", 1), ("t", 2), ("b", 2))
SLOT = {"chip": 0, "near": 1, "far": 2}
NEV = 112

SCRATCH = {
    "qs": ("sbuf", [128, 256], "bfloat16"),
    "kv": ("sbuf", [128, 512], "bfloat16"),
    "land": ("sbuf", [128, 3 * 512], "bfloat16"),
    "ones": ("sbuf", [128, 128], "bfloat16"),
    "ident": ("sbuf", [128, 128], "bfloat16"),
    "pw": ("sbuf", [128, NH * 512], "bfloat16"),
    "pt": ("sbuf", [128, NH * 512], "bfloat16"),
    "dg": ("sbuf", [128, NH * 512], "bfloat16"),
    "ob": ("sbuf", [128, NH * 512], "bfloat16"),
    "st": ("sbuf", [128, 48], "float32"),
    "ysb": ("sbuf", [128, 256], "bfloat16"),
    "s00": ("psum", [128, 512], "float32"),
    "s01": ("psum", [128, 512], "float32"),
    "s10": ("psum", [128, 512], "float32"),
    "s11": ("psum", [128, 512], "float32"),
    "t0": ("psum", [128, 1024], "bfloat16"),
    "t1": ("psum", [128, 1024], "bfloat16"),
    "o0": ("psum", [128, 512], "float32"),
    "o1": ("psum", [128, 512], "float32"),
}
SEMAPHORES = ["sent"] + ["arr%d%d" % (j, p) for j in range(3) for p in range(3)] + ["e%d" % i for i in range(NEV)]


def rank_program(g, core, T, topo):
    if T.rank_of(core) is None:
        return
    EXP, IDN = ActivationFunctionType.Exp, ActivationFunctionType.Identity
    MUL, MAX = AluOpType.mult, AluOpType.max

    def same_chip(a, b):
        return (topo.host(a), topo.chip(a)) == (topo.host(b), topo.chip(b))

    def place(src, dst):
        if same_chip(src, dst):
            return "chip"
        return "near" if topo.die(src) == topo.die(dst) else "far"

    def engines(src, dst):
        m = topo.mask(src, dst)
        if same_chip(src, dst):
            off = 0
            for d in T.cores:
                if not same_chip(src, d):
                    off |= topo.mask(src, d)
            return (m & ~off) or m
        bits = [1 << i for i in range(m.bit_length()) if (m >> i) & 1]
        half = len(bits) // 2
        return sum(bits[:half] if place(src, dst) == "near" else bits[half:])

    def count(m):
        return bin(m).count("1")

    peer = {place(core, d): d for d in T.cores if d != core}

    queues = {"pe": g.tensor, "dve": g.vector, "act": g.scalar, "sp": g.sync, "g": g}
    ops, evs = [], []

    def ev(val, sem=None):
        e = {"n": len(evs), "val": val, "sem": sem, "used": False}
        evs.append(e)
        return e

    def op(q, fn, waits=(), sig=None, inc=1):
        ops.append((q, fn, [w for w in waits if w is not None], sig, inc))

    def mm(out, lhsT, rhs, start, stop):
        return lambda: g.tensor.matmul(out, lhsT, rhs, start, stop)

    def tr(out, in_):
        return lambda: g.tensor.transpose(out, in_, T.ident[:])

    def tsc(out, in0, s1):
        return lambda: g.vector.tensor_scalar(out, in0, s1, None, MUL)

    def cpy(out, in_):
        return lambda: g.vector.tensor_copy(out, in_)

    def actv(out, in_, func, bias, scale, acc=None):
        return lambda: g.scalar.activation(out, in_, func, bias=bias, scale=scale, accum_out=acc)

    def col(kind, s, h):
        c = 8 * kind + 2 * s + h
        return T.st[:, c:c + 1]

    ld_k, ld_v, ld_q = ev(16), ev(16), ev(16)
    op("sp", lambda: g.sync.dma_start(T.kv[:, 0:256], T.k[:, :]), sig=ld_k, inc=16)
    op("sp", lambda: g.sync.dma_start(T.qs[:], T.q[:, :]), sig=ld_q, inc=16)
    op("sp", lambda: g.sync.dma_start(T.kv[:, 256:512], T.v[:, :]), sig=ld_v, inc=16)

    e_ones, e_id = ev(1), ev(1)
    op("dve", lambda: g.vector.memset(T.ones[:], 1.0), sig=e_ones)
    op("g", lambda: g.affine_select(T.ident[:], T.ones[:], [[-1, 128]], AluOpType.is_equal, 0.0, 0, 1), [e_ones], e_id)

    def send(call):
        parts = []
        for where, p in call:
            d = peer[where]
            rid, pid = topo.addr(d, core)
            a, b = PIECES[p]
            j = SLOT[where]
            parts.append((T.land[:, 512 * j + a:512 * j + b], T.kv[:, a:b], T.sem["arr%d%d" % (j, p)], pid, rid, engines(core, d)))
        if len(parts) == 1:
            o, i, sem, pid, rid, m = parts[0]
            return lambda: g.remote_dma(o, i, sem, T.sem.sent, pid, rid, m)
        return lambda: g.remote_dma_fused(
            [RemoteDMATransfer(dst_ids=[DstId(rid=rid, pnc=pid)], dma_engine_mask=m, remote_sem=sem, src=i, dst=o)
             for o, i, sem, pid, rid, m in parts], local_sem=T.sem.sent)

    total = 0
    for call in SENDS:
        lo = min(PIECES[p][0] for _, p in call)
        hi = max(PIECES[p][1] for _, p in call)
        op("g", send(call), [ld_k if lo < 256 else None, ld_v if hi > 256 else None])
        total += sum(count(engines(core, peer[where])) for where, _ in call)
    e_sent = ev(total, T.sem.sent)

    arr = {(w, p): ev(count(engines(peer[w], core)), T.sem["arr%d%d" % (SLOT[w], p)]) for call in SENDS for w, p in call}

    def landed(b, c):
        return [e for (w, p), e in arr.items() if w == b and PIECES[p][0] <= c < PIECES[p][1]][0]

    def k_of(b, h):
        if b == "own":
            return T.kv[:, 128 * h:128 * h + 128], ld_k
        o = 512 * SLOT[b] + 128 * h
        return T.land[:, o:o + 128], landed(b, 128 * h)

    def v_of(b, h):
        if b == "own":
            return T.kv[:, 256 + 128 * h:384 + 128 * h], ld_v
        o = 512 * SLOT[b] + 256 + 128 * h
        return T.land[:, o:o + 128], landed(b, 256 + 128 * h)

    H = range(NH)
    TB = [T.t0, T.t1]
    OB = [T.o0, T.o1]
    e_st, e_max, e_mcol, e_exp, e_f, e_l, e_t, e_cp, e_dg, e_o, e_ob = {}, {}, {}, {}, {}, {}, {}, {}, {}, {}, {}
    nst = len(STAGES)
    POS = [128 * sum(len(STAGES[i]) for i in range(s)) for s in range(nst)]

    def front(s):
        blocks = STAGES[s]
        nb, pos = len(blocks), POS[s]
        w = 128 * nb
        SB = [T["s%d%d" % (s % 2, h)] for h in H]
        for h in H:
            e_st[s, h] = ev(nb)
            for i, b in enumerate(blocks):
                ap, e = k_of(b, h)
                op("pe", mm(SB[h][:, 128 * i:128 * i + 128], T.qs[:, 128 * h:128 * h + 128], ap, True, True),
                   [ld_q, e, e_mcol.get((s - 1, h))], e_st[s, h])
        for h in H:
            e_max[s, h] = ev(1)
            op("dve", (lambda o, i: lambda: g.vector.tensor_reduce(o, i, AxisListType.X, MAX, negate=True))(
                col(0, s, h), SB[h][:, 0:w + (1 if s else 0)]), [e_st[s, h], e_mcol.get((s - 1, h))], e_max[s, h])
        if s < nst - 1:
            nw = 128 * len(STAGES[s + 1])
            for h in H:
                e_mcol[s, h] = ev(1)
                op("dve", tsc(T["s%d%d" % ((s + 1) % 2, h)][:, nw:nw + 1], col(0, s, h), -1.0),
                   [e_max[s, h], e_exp.get((s - 1, h))], e_mcol[s, h])
        for h in H:
            e_exp[s, h] = ev(1)
            o = 512 * h + pos
            op("act", actv(T.pw[:, o:o + w], SB[h][:, 0:w], EXP, col(0, s, h), 1.0, col(1 if s else 3, s, h)),
               [e_max[s, h]], e_exp[s, h])
        if s:
            for h in H:
                e_f[s, h] = ev(1)
                op("act", actv(col(2, s, h), col(0, s - 1, h), EXP, col(0, s, h), -1.0), [e_max[s, h], e_max[s - 1, h]], e_f[s, h])
            for h in H:
                e_l[s, h] = ev(1)
                op("act", actv(col(3, s, h), col(3, s - 1, h), IDN, col(1, s, h), col(2, s, h)),
                   [e_f[s, h], e_exp[s, h], e_l[s - 1, h]], e_l[s, h])
        else:
            for h in H:
                e_l[s, h] = e_exp[s, h]

    def turn(s):
        nb, pos = len(STAGES[s]), POS[s]
        w = 128 * nb
        for h in H:
            e_t[s, h] = ev(nb)
            for i in range(nb):
                o = 512 * h + pos + 128 * i
                op("pe", tr(TB[h][:, 128 * i:128 * i + 128], T.pw[:, o:o + 128]), [e_exp[s, h], e_id, e_cp.get((s - 1, h))], e_t[s, h])
        for h in H:
            e_cp[s, h] = ev(1)
            o = 512 * h + pos
            op("dve", cpy(T.pt[:, o:o + w], TB[h][:, 0:w]), [e_t[s, h]], e_cp[s, h])
            if s:
                e_dg[s, h] = ev(1)
                o = 512 * h + 128 * s
                op("dve", tsc(T.dg[:, o:o + 128], T.ident[:], col(2, s, h)), [e_f[s, h], e_id], e_dg[s, h])

    def back(s):
        blocks = STAGES[s]
        nb, pos = len(blocks), POS[s]
        for h in H:
            e_o[s, h] = ev(nb + (1 if s else 0))
            if s:
                o = 512 * h + 128 * s
                op("pe", mm(OB[h][:, 0:128], T.dg[:, o:o + 128], T.ob[:, o - 128:o], True, False),
                   [e_dg[s, h], e_ob[s - 1, h]], e_o[s, h])
            for i, b in enumerate(blocks):
                ap, e = v_of(b, h)
                o = 512 * h + pos + 128 * i
                op("pe", mm(OB[h][:, 0:128], T.pt[:, o:o + 128], ap, s == 0 and i == 0, i == nb - 1), [e_cp[s, h], e], e_o[s, h])
        if s < nst - 1:
            for h in H:
                e_ob[s, h] = ev(1)
                o = 512 * h + 128 * s
                op("dve", cpy(T.ob[:, o:o + 128], OB[h][:, 0:128]), [e_o[s, h]], e_ob[s, h])
        else:
            e_r, e_y0, e_y1, e_done = ev(1), ev(1), ev(1), ev(16)
            c = 24 + 2 * s
            op("dve", lambda: g.vector.reciprocal(T.st[:, 40:42], T.st[:, c:c + 2]), [e_l[s, 0], e_l[s, 1]], e_r)
            op("act", actv(T.ysb[:, 0:128], OB[0][:, 0:128], IDN, 0.0, T.st[:, 40:41]), [e_o[s, 0], e_r], e_y0)
            op("dve", tsc(T.ysb[:, 128:256], OB[1][:, 0:128], T.st[:, 41:42]), [e_o[s, 1], e_r], e_y1)
            op("sp", lambda: g.sync.dma_start(T.y[:, :], T.ysb[:]), [e_y0, e_y1], e_done, 16)
            op("sp", None, [e_done])

    part = {"f": front, "t": turn, "b": back}
    for name, s in ORDER:
        part[name](s)
    op("g", None, [e_sent])

    for _, _, waits, _, _ in ops:
        for e in waits:
            e["used"] = True
    free = [0]
    for e in evs:
        if e["used"] and e["sem"] is None:
            e["sem"] = T.sem["e%d" % free[0]]
            free[0] += 1
    seen = set()
    for q, fn, waits, sig, inc in ops:
        for e in waits:
            if (q, e["n"]) not in seen:
                seen.add((q, e["n"]))
                queues[q].wait_ge(e["sem"], e["val"])
        if fn is not None:
            ins = fn()
            if sig is not None and sig["used"]:
                ins.then_inc(sig["sem"], inc)
